import numpy as np
import ml_dtypes


def mxq(x, axis, fmt="e4m3"):
    dtype, down = {"e4m3": (ml_dtypes.float8_e4m3fn, 7), "e5m2": (ml_dtypes.float8_e5m2, 14)}[fmt]
    v = np.moveaxis(np.asarray(x, np.float32).astype(ml_dtypes.bfloat16).astype(np.float64), axis, -1)
    blocks = v.reshape(v.shape[:-1] + (-1, 32))
    amax = np.abs(blocks).max(-1, keepdims=True)
    byte = np.maximum(np.where(amax > 0, np.frexp(amax)[1] - 1 + 127, 0) - down, 1)
    scale = np.exp2(byte - 127.0)
    codes = (blocks / scale).astype(np.float32).astype(dtype).astype(np.float64)
    return np.moveaxis((codes * scale).reshape(v.shape), -1, axis)


WIDE = False


def mx_kscale(k):
    if not WIDE:
        return np.ones(k)
    levels = np.array([10, -10, 5, -5, 0])
    if k % 512:
        return np.exp2(np.random.permutation(np.resize(levels, k // 32))).repeat(32)
    a = np.empty((k // 512, 16))
    for p in range(k // 512):
        a[p, :8] = np.random.permutation(np.resize(levels, 8))
        for g in range(8):
            far = levels[np.abs(levels - a[p, g]) >= 10]
            a[p, g + 8] = far[np.random.randint(len(far))]
    return np.exp2(a.ravel()).repeat(32)


def f64(x):
    return np.asarray(x).astype(np.float64)


def striped(idx):
    return np.tile(idx.reshape(-1, 16).T, (8, 1)).astype(np.uint16)


def unstriped(offs):
    return offs[:16].T.reshape(-1).astype(np.int64)


def striped8(idx):
    return np.concatenate([x.reshape(-1, 16).T for x in idx]).astype(np.uint16)


def runs(offs, k):
    lists = np.stack([offs[16 * r : 16 * r + 16].T.reshape(-1) for r in range(8)]).astype(np.int64)
    return lists[np.arange(k) % 512 // 64]


def pack_weight(w):
    k, n = w.shape
    w = f64(np.asarray(w, np.float32).astype(ml_dtypes.bfloat16)).reshape(k // 32, 32, n)
    amax = np.abs(w).max(1)
    byte = np.clip(np.where(amax > 0, np.frexp(amax)[1] - 1 + 127 - 7, 1), 1, 254)
    scaled = (w * np.exp2(127.0 - byte)[:, None, :]).reshape(k, n).astype(np.float32)
    words = np.ascontiguousarray(scaled.reshape(k // 512, 128, 4, n).transpose(0, 1, 3, 2)).astype(ml_dtypes.float8_e4m3fn).view(np.uint8)
    return words, np.ascontiguousarray(byte.astype(np.uint8).reshape(k // 512, 16, n))


def unpack_weight(words, scales):
    g, p, n, _ = words.shape
    vals = np.ascontiguousarray(words).view(ml_dtypes.float8_e4m3fn).astype(np.float64) * np.repeat(np.exp2(scales.astype(np.float64) - 127.0), 8, axis=1)[..., None]
    return vals.transpose(0, 1, 3, 2).reshape(g * 512, n)

def planes(y):
    n, m = y.shape
    v = y.astype(np.float32).astype(ml_dtypes.bfloat16).astype(np.float64).reshape(n // 32, 32, m)
    top = np.abs(v).max(1)
    byte = np.clip(np.where(top > 0, np.frexp(top)[1] - 1 + 127 - 7, 1), 1, 254)
    codes = (v * np.exp2(127.0 - byte)[:, None, :]).reshape(n, m).astype(np.float32).astype(ml_dtypes.float8_e4m3fn).view(np.uint8)
    words = codes.reshape(n // 512, 128, 4, m).transpose(0, 1, 3, 2)
    return np.ascontiguousarray(words), np.ascontiguousarray(byte.astype(np.uint8).reshape(n // 512, 16, m))


K, T, S, N, H, U = 512, 2048, 512, 512, 512, 1024


def setup_inputs():
    n = np.random.standard_normal
    s = mx_kscale(K)[:, None]
    u = mx_kscale(H)
    packed_xT = pack_weight(n((K, T)) * s)
    packed_w1 = pack_weight(n((K, H)) / np.sqrt(K) / s)
    packed_w2 = pack_weight(n((H, N)) / np.sqrt(H) / u[:, None])
    return {
        "x_words": packed_xT[0],
        "x_scales": packed_xT[1],
        "w1_words": packed_w1[0],
        "w1_scales": packed_w1[1],
        "gn": (np.random.uniform(0.5, 1.5, (H, 1)) * u[:, None]).astype(np.float32),
        "w2_words": packed_w2[0],
        "w2_scales": packed_w2[1],
        "mem": n((N, U)).astype(np.float32),
        "offs": striped(np.random.permutation(T)[:S]),
        "p1": striped8(np.stack([np.random.permutation(S) for _ in range(8)])),
        "p2": striped8(np.stack([np.random.permutation(S) for _ in range(8)])),
        "p3": striped8(np.stack([np.random.permutation(S) for _ in range(8)])),
        "p4": striped8(np.stack([np.random.permutation(S) for _ in range(8)])),
        "slot": striped8(np.stack([np.random.permutation(U)[:S] for _ in range(8)])),
    }


def reference(x_words, x_scales, w1_words, w1_scales, gn, w2_words, w2_scales, mem, offs, p1, p2, p3, p4, slot):
    xq = unpack_weight(x_words, x_scales)[:, unstriped(offs)]
    y = unpack_weight(w1_words, w1_scales).T @ xq
    a = y[np.arange(H)[:, None], runs(p1, H)]
    b = y[np.arange(H)[:, None], runs(p2, H)]
    m1 = np.maximum(np.minimum(y, a), np.minimum(np.maximum(y, a), b))
    c = m1[np.arange(H)[:, None], runs(p3, H)]
    d = m1[np.arange(H)[:, None], runs(p4, H)]
    z = f64(gn) * (0.5 * y - (np.maximum(np.minimum(m1, c), np.minimum(np.maximum(m1, c), d))))
    h = unpack_weight(w2_words, w2_scales).T @ mxq(z, 0, "e4m3")
    out = f64(mem).copy()
    out[np.arange(N)[:, None], runs(slot, N)] = h
    return (out,) + planes(out)

@@ -1,0 +1,207 @@
+from contextlib import ExitStack
+
+import concourse.mybir as mybir
+from concourse.masks import make_identity
+
+K, T, S, N, H, U = 512, 2048, 512, 512, 512, 1024
+FLOPS = 2 * K * H * S + 2 * H * N * S
+
+F32 = mybir.dt.float32
+BF16 = mybir.dt.bfloat16
+I32 = mybir.dt.int32
+U32 = mybir.dt.uint32
+U16 = mybir.dt.uint16
+U8 = mybir.dt.uint8
+FP8X4 = mybir.dt.float8_e4m3fn_x4
+ALU = mybir.AluOpType
+COPY = mybir.ActivationFunctionType.Copy
+
+P = 128
+PACK = 4
+CHUNK = 256
+LIST_COLS = S // 16
+VEC_COLS = 640
+
+
+def tile_picked_medfilt2_none_po_kernel(tc, x_words, x_scales, w1_words, w1_scales, gn, w2_words, w2_scales, mem,
+        offs, p1, p2, p3, p4, slot, out_0, out_1, out_2):
+    nc = tc.nc
+    with ExitStack() as ctx:
+        lists = ctx.enter_context(tc.tile_pool(name="lists", bufs=1))
+        keep = ctx.enter_context(tc.tile_pool(name="keep", bufs=1))
+        shared = ctx.enter_context(tc.tile_pool(name="shared", bufs=1))
+        ring = ctx.enter_context(tc.tile_pool(name="ring", bufs=3))
+        psum = ctx.enter_context(tc.psum_pool(name="psum", bufs=8))
+
+        def load_list(src, name):
+            tile = lists.tile([P, LIST_COLS], U16, name=name)
+            nc.sync.dma_start(tile[:], src)
+            return tile
+
+        def load_scales(src, plane, queues):
+            for q, queue in enumerate(queues):
+                queue.dma_start(plane[32 * q : 32 * q + 4, :].bitcast(I32), src[0, 4 * q : 4 * q + 4, :].bitcast(I32))
+
+        def words_of(src):
+            return src[0].rearrange("p n t -> p (n t)").bitcast(I32)
+
+        def deal(raw, dtype, name):
+            dealt = keep.tile([P, PACK, P], dtype, name=name, align_bytes=64)
+            nc.vector.tensor_copy(dealt[:], raw[:].rearrange("p (m t) -> p t m", t=PACK))
+            return dealt
+
+        offs_l = load_list(offs, "offs_l")
+        p1_l = load_list(p1, "p1_l")
+        p2_l = load_list(p2, "p2_l")
+        p3_l = load_list(p3, "p3_l")
+        p4_l = load_list(p4, "p4_l")
+        slot_l = load_list(slot, "slot_l")
+        gain = keep.tile([P, PACK], F32)
+        nc.sync.dma_start(gain[:], gn.rearrange("(p t) o -> p (t o)", t=PACK))
+        w1_raw = shared.tile([P, H], I32, offset=16384)
+        nc.sync.dma_start(w1_raw[:], words_of(w1_words))
+        x_plane = keep.tile([P, T], U8)
+        nc.vector.memset(x_plane[:].bitcast(I32), 0)
+        load_scales(x_scales, x_plane, [nc.sync] * 4)
+        x_table = shared.tile([P, T], I32, offset=2048)
+        nc.sync.dma_start(x_table[:], words_of(x_words))
+        w1_plane = keep.tile([P, H], U8)
+        nc.gpsimd.memset(w1_plane[:].bitcast(I32), 0)
+        load_scales(w1_scales, w1_plane, [nc.sync] * 4)
+        w2_plane = keep.tile([P, N], U8)
+        nc.vector.memset(w2_plane[:].bitcast(I32), 0)
+        load_scales(w2_scales, w2_plane, [nc.sync] * 4)
+
+        y_win = [keep.tile([P, 2 * S], F32, name="y_win%d" % t) for t in range(PACK)]
+        nc.vector.memset(y_win[0][:, S:], 0.0)
+        for t in range(1, PACK):
+            nc.scalar.activation(y_win[t][:, S:], y_win[0][:, S:], COPY)
+        ident = keep.tile([P, P], F32)
+        make_identity(nc, ident[:])
+
+        w1_codes = deal(w1_raw, I32, "w1_codes")
+        x_bytes = keep.tile([P, S], U8, align_bytes=64)
+        nc.vector.tensor_copy(x_bytes[:], x_plane[:].indirect(offs_l[:]))
+        x_codes = shared.tile([P, S], U32, offset=12288, align_bytes=64)
+        for c in range(S // CHUNK):
+            nc.vector.tensor_copy(x_codes[:, c * CHUNK : (c + 1) * CHUNK],
+                                  x_table[:].bitcast(U32).indirect(offs_l[:, c * CHUNK // 16 : (c + 1) * CHUNK // 16]))
+            if c == 0:
+                w1_bytes = deal(w1_plane, U8, "w1_bytes")
+        w2_raw = shared.tile([P, N], I32, offset=16384)
+        nc.sync.dma_start(w2_raw[:], words_of(w2_words))
+        w2_codes = deal(w2_raw, I32, "w2_codes")
+        w2_bytes = deal(w2_plane, U8, "w2_bytes")
+
+        y_own = [keep.tile([P, S], F32, name="y_own%d" % t) for t in range(PACK)]
+        y_half = [keep.tile([P, S], F32, name="y_half%d" % t) for t in range(PACK)]
+        for t in range(PACK):
+            width = CHUNK if t == 0 else S
+            for c in range(S // width):
+                cols = slice(c * width, (c + 1) * width)
+                bank = psum.tile([P, width], F32, name="bank", tag="bank")
+                nc.tensor.matmul_mx(bank[:], lhsT=w1_codes[:, t, :].bitcast(FP8X4), lhsT_scale=w1_bytes[:, t, :],
+                                    rhs=x_codes[:, cols].bitcast(FP8X4), rhs_scale=x_bytes[:, cols], start=True, stop=True)
+                nc.scalar.activation(y_win[t][:, cols], bank[:], COPY, scale=gain[:, t : t + 1])
+                nc.scalar.activation(y_own[t][:, cols], bank[:], COPY, scale=gain[:, t : t + 1])
+
+        page = [shared.tile([P, U], F32, name="page%d" % t, offset=4096 * t) for t in range(PACK)]
+        mem_rows = mem.rearrange("(p t) u -> p t u", t=PACK)
+        for t in range(PACK):
+            nc.sync.dma_start(page[t][:], mem_rows[:, t, :])
+
+        def median_steps(tiles, windows, own, list_a, list_b, steps, width):
+            da, db, low = {}, {}, {}
+            for t in tiles:
+                da[t] = ring.tile([P, width], F32, name="da", tag="da%d" % width)
+                nc.vector.tensor_tensor(da[t][:], windows[t][:].indirect(list_a), own[t], ALU.subtract)
+                db[t] = ring.tile([P, width], F32, name="db", tag="db%d" % width)
+                nc.vector.tensor_tensor(db[t][:], windows[t][:].indirect(list_b), own[t], ALU.subtract)
+            for t in tiles:
+                low[t] = ring.tile([P, width], F32, name="low", tag="low%d" % width)
+                nc.vector.scalar_tensor_tensor(low[t][:], db[t][:], 0.0, da[t][:], ALU.min, ALU.max)
+            for t in tiles:
+                nc.vector.scalar_tensor_tensor(steps[t], db[t][:], 0.0, low[t][:], ALU.max, ALU.min)
+
+        step1 = [keep.tile([P, S], F32, name="step1_%d" % t) for t in range(PACK)]
+        m1_win = [keep.tile([P, S], F32, name="m1_win%d" % t) for t in range(PACK)]
+        m1_own = [keep.tile([P, S], F32, name="m1_own%d" % t) for t in range(PACK)]
+        for pair in ((0, 1), (2, 3)):
+            median_steps(pair, y_win, [y[:] for y in y_own], p1_l[:], p2_l[:], [s[:] for s in step1], S)
+            for t in pair:
+                turned = psum.tile([P, S // P, P], F32, name="turned", tag="bank")
+                for b in range(S // P):
+                    block = slice(b * P, (b + 1) * P)
+                    nc.tensor.matmul(turned[:, b, :], y_own[t][:, block], ident[:], start=True, stop=False, is_transpose=True)
+                    nc.tensor.matmul(turned[:, b, :], step1[t][:, block], ident[:], start=False, stop=True, is_transpose=True)
+                m1_turned = ring.tile([P, S // P, P], F32, name="m1_turned")
+                nc.scalar.copy(m1_turned[:], turned[:])
+                m1_back = psum.tile([P, S], F32, name="m1_back", tag="bank")
+                for b in range(S // P):
+                    nc.tensor.transpose(m1_back[:, b * P : (b + 1) * P], m1_turned[:, b, :], ident[:])
+                nc.scalar.copy(m1_win[t][:], m1_back[:])
+                nc.scalar.copy(m1_own[t][:], m1_back[:])
+        for t in range(PACK):
+            nc.scalar.activation(y_half[t][:], y_own[t][:], COPY, scale=0.5)
+
+        h = {}
+        for c in range(S // CHUNK):
+            cols = slice(c * CHUNK, (c + 1) * CHUNK)
+            entries = slice(c * CHUNK // 16, (c + 1) * CHUNK // 16)
+            step2 = [keep.tile([P, CHUNK], F32, name="step2_%d_%d" % (c, t)) for t in range(PACK)]
+            z_turned = [psum.tile([P, PACK, P], F32, name="z_turned", tag="bank") for b in range(CHUNK // P)]
+            for pair in ((0, 1), (2, 3)):
+                median_steps(pair, m1_win, [m[:, cols] for m in m1_own], p3_l[:, entries], p4_l[:, entries],
+                             [s[:] for s in step2], CHUNK)
+                for t in pair:
+                    for b in range(CHUNK // P):
+                        block = slice(c * CHUNK + b * P, c * CHUNK + (b + 1) * P)
+                        terms = (y_half[t][:, block], step1[t][:, block], step2[t][:, b * P : (b + 1) * P])
+                        for i, term in enumerate(terms):
+                            nc.tensor.matmul(z_turned[b][:, t, :], term, ident[:], start=(i == 0), stop=(i == len(terms) - 1),
+                                             is_transpose=True)
+            z_back = psum.tile([P, CHUNK // P, 2, P], F32, name="z_back", tag="bank")
+            for b in range(CHUNK // P):
+                z_pairs = ring.tile([P, 2, P, 2], BF16, name="z_pairs")
+                nc.scalar.activation(z_pairs[:], z_turned[b][:].rearrange("j (u e) p -> j u p e", e=2), COPY, scale=-1.0)
+                z_words = z_pairs[:].rearrange("j u p e -> j u (p e)").bitcast(F32)
+                for u in range(2):
+                    nc.tensor.transpose(z_back[:, b, u, :], z_words[:, u, :], ident[:])
+            z_bf = ring.tile([P, CHUNK * PACK], BF16, name="z_bf", align_bytes=64)
+            nc.scalar.copy(z_bf[:].bitcast(F32).rearrange("p (b j u) -> p b j u", u=2, j=P),
+                           z_back[:].rearrange("p b u j -> p b j u"))
+            z_codes = ring.tile([P, CHUNK], U32, name="z_codes", align_bytes=64)
+            z_bytes = ring.tile([P, CHUNK], U8, name="z_bytes", align_bytes=64)
+            nc.vector.quantize_mx(z_codes[:].bitcast(FP8X4), z_bytes[:], z_bf[:])
+            for t in range(PACK):
+                bank = psum.tile([P, CHUNK], F32, name="bank", tag="bank")
+                nc.tensor.matmul_mx(bank[:], lhsT=w2_codes[:, t, :].bitcast(FP8X4), lhsT_scale=w2_bytes[:, t, :],
+                                    rhs=z_codes[:].bitcast(FP8X4), rhs_scale=z_bytes[:], start=True, stop=True)
+                h[c, t] = keep.tile([P, CHUNK], F32, name="h%d_%d" % (c, t))
+                nc.scalar.copy(h[c, t][:], bank[:])
+
+        out_rows = out_0.rearrange("(p t) u -> p t u", t=PACK)
+        rounded = keep.tile([P, PACK, U], BF16)
+        for c, t in ((0, 0), (0, 1), (0, 2), (1, 0), (1, 1), (1, 2), (0, 3), (1, 3)):
+            entries = slice(c * CHUNK // 16, (c + 1) * CHUNK // 16)
+            nc.vector.tensor_copy(page[t][:].indirect(slot_l[:, entries]), h[c, t][:])
+            if c == 1:
+                nc.sync.dma_start(out_rows[:, t, :], page[t][:])
+                if t < PACK - 1:
+                    nc.scalar.copy(rounded[:, t, :], page[t][:])
+                else:
+                    nc.vector.tensor_copy(rounded[:, t, :VEC_COLS], page[t][:, :VEC_COLS])
+                    nc.scalar.copy(rounded[:, t, VEC_COLS:], page[t][:, VEC_COLS:])
+        grouped = keep.tile([P, U, PACK], BF16, align_bytes=64)
+        half = U // 2
+        nc.vector.tensor_copy(grouped[:, :half, :], rounded[:, :, :half].rearrange("p t c -> p c t"))
+        nc.vector.tensor_copy(grouped[:, half:VEC_COLS, :], rounded[:, :, half:VEC_COLS].rearrange("p t c -> p c t"))
+        nc.scalar.copy(grouped[:, VEC_COLS:, :], rounded[:, :, VEC_COLS:].rearrange("p t c -> p c t"))
+        out_codes = keep.tile([P, U], U32, align_bytes=64)
+        out_bytes = keep.tile([P, U], U8, align_bytes=64)
+        for cols in (slice(0, half), slice(half, U)):
+            nc.vector.quantize_mx(out_codes[:, cols].bitcast(FP8X4), out_bytes[:, cols],
+                                  grouped[:, cols, :].rearrange("p c t -> p (c t)"))
+            nc.sync.dma_start(words_of(out_1)[:, cols], out_codes[:, cols].bitcast(I32))
+        for q in range(4):
+            nc.scalar.dma_start(out_2[0, 4 * q : 4 * q + 4, :].bitcast(I32), out_bytes[32 * q : 32 * q + 4, :].bitcast(I32))

@@ -20,7 +20,7 @@ P = 128
 PACK = 4
 CHUNK = 256
 LIST_COLS = S // 16
-VEC_COLS = 640
+VEC_COLS = 576
 
 
 def tile_picked_medfilt2_none_po_kernel(tc, x_words, x_scales, w1_words, w1_scales, gn, w2_words, w2_scales, mem,
@@ -58,7 +58,7 @@ def tile_picked_medfilt2_none_po_kernel(tc, x_words, x_scales, w1_words, w1_scal
         slot_l = load_list(slot, "slot_l")
         gain = keep.tile([P, PACK], F32)
         nc.sync.dma_start(gain[:], gn.rearrange("(p t) o -> p (t o)", t=PACK))
-        w1_raw = shared.tile([P, H], I32, offset=16384)
+        w1_raw = keep.tile([P, H], I32)
         nc.sync.dma_start(w1_raw[:], words_of(w1_words))
         x_plane = keep.tile([P, T], U8)
         nc.vector.memset(x_plane[:].bitcast(I32), 0)
@@ -68,6 +68,8 @@ def tile_picked_medfilt2_none_po_kernel(tc, x_words, x_scales, w1_words, w1_scal
         w1_plane = keep.tile([P, H], U8)
         nc.gpsimd.memset(w1_plane[:].bitcast(I32), 0)
         load_scales(w1_scales, w1_plane, [nc.sync] * 4)
+        w2_raw = keep.tile([P, N], I32)
+        nc.sync.dma_start(w2_raw[:], words_of(w2_words))
         w2_plane = keep.tile([P, N], U8)
         nc.vector.memset(w2_plane[:].bitcast(I32), 0)
         load_scales(w2_scales, w2_plane, [nc.sync] * 4)
@@ -88,8 +90,6 @@ def tile_picked_medfilt2_none_po_kernel(tc, x_words, x_scales, w1_words, w1_scal
                                   x_table[:].bitcast(U32).indirect(offs_l[:, c * CHUNK // 16 : (c + 1) * CHUNK // 16]))
             if c == 0:
                 w1_bytes = deal(w1_plane, U8, "w1_bytes")
-        w2_raw = shared.tile([P, N], I32, offset=16384)
-        nc.sync.dma_start(w2_raw[:], words_of(w2_words))
         w2_codes = deal(w2_raw, I32, "w2_codes")
         w2_bytes = deal(w2_plane, U8, "w2_bytes")
 
@@ -110,79 +110,93 @@ def tile_picked_medfilt2_none_po_kernel(tc, x_words, x_scales, w1_words, w1_scal
         for t in range(PACK):
             nc.sync.dma_start(page[t][:], mem_rows[:, t, :])
 
-        def median_steps(tiles, windows, own, list_a, list_b, steps, width):
-            da, db, low = {}, {}, {}
-            for t in tiles:
-                da[t] = ring.tile([P, width], F32, name="da", tag="da%d" % width)
-                nc.vector.tensor_tensor(da[t][:], windows[t][:].indirect(list_a), own[t], ALU.subtract)
-                db[t] = ring.tile([P, width], F32, name="db", tag="db%d" % width)
-                nc.vector.tensor_tensor(db[t][:], windows[t][:].indirect(list_b), own[t], ALU.subtract)
-            for t in tiles:
-                low[t] = ring.tile([P, width], F32, name="low", tag="low%d" % width)
-                nc.vector.scalar_tensor_tensor(low[t][:], db[t][:], 0.0, da[t][:], ALU.min, ALU.max)
-            for t in tiles:
-                nc.vector.scalar_tensor_tensor(steps[t], db[t][:], 0.0, low[t][:], ALU.max, ALU.min)
+        def turned_sum(out, terms):
+            for i, term in enumerate(terms):
+                nc.tensor.matmul(out, term, ident[:], start=(i == 0), stop=(i == len(terms) - 1), is_transpose=True)
 
-        step1 = [keep.tile([P, S], F32, name="step1_%d" % t) for t in range(PACK)]
+        blocks = [slice(b * P, (b + 1) * P) for b in range(S // P)]
         m1_win = [keep.tile([P, S], F32, name="m1_win%d" % t) for t in range(PACK)]
         m1_own = [keep.tile([P, S], F32, name="m1_own%d" % t) for t in range(PACK)]
-        for pair in ((0, 1), (2, 3)):
-            median_steps(pair, y_win, [y[:] for y in y_own], p1_l[:], p2_l[:], [s[:] for s in step1], S)
-            for t in pair:
-                turned = psum.tile([P, S // P, P], F32, name="turned", tag="bank")
-                for b in range(S // P):
-                    block = slice(b * P, (b + 1) * P)
-                    nc.tensor.matmul(turned[:, b, :], y_own[t][:, block], ident[:], start=True, stop=False, is_transpose=True)
-                    nc.tensor.matmul(turned[:, b, :], step1[t][:, block], ident[:], start=False, stop=True, is_transpose=True)
-                m1_turned = ring.tile([P, S // P, P], F32, name="m1_turned")
-                nc.scalar.copy(m1_turned[:], turned[:])
-                m1_back = psum.tile([P, S], F32, name="m1_back", tag="bank")
-                for b in range(S // P):
-                    nc.tensor.transpose(m1_back[:, b * P : (b + 1) * P], m1_turned[:, b, :], ident[:])
-                nc.scalar.copy(m1_win[t][:], m1_back[:])
-                nc.scalar.copy(m1_own[t][:], m1_back[:])
-        for t in range(PACK):
-            nc.scalar.activation(y_half[t][:], y_own[t][:], COPY, scale=0.5)
+        step1 = [keep.tile([P, S], F32, name="step1_%d" % t) for t in range(PACK)]
+        step2 = [keep.tile([P, S], F32, name="step2_%d" % t) for t in range(PACK)]
+        diff_a = [keep.tile([P, S], F32, name="diff_a%d" % i) for i in range(2)]
+        diff_b = [keep.tile([P, S], F32, name="diff_b%d" % i) for i in range(2)]
+        low = [keep.tile([P, S], F32, name="low%d" % i) for i in range(2)]
+        z_turned, h, held_bank = {}, {}, []
 
-        h = {}
-        for c in range(S // CHUNK):
-            cols = slice(c * CHUNK, (c + 1) * CHUNK)
-            entries = slice(c * CHUNK // 16, (c + 1) * CHUNK // 16)
-            step2 = [keep.tile([P, CHUNK], F32, name="step2_%d_%d" % (c, t)) for t in range(PACK)]
-            z_turned = [psum.tile([P, PACK, P], F32, name="z_turned", tag="bank") for b in range(CHUNK // P)]
-            for pair in ((0, 1), (2, 3)):
-                median_steps(pair, m1_win, [m[:, cols] for m in m1_own], p3_l[:, entries], p4_l[:, entries],
-                             [s[:] for s in step2], CHUNK)
-                for t in pair:
-                    for b in range(CHUNK // P):
-                        block = slice(c * CHUNK + b * P, c * CHUNK + (b + 1) * P)
-                        terms = (y_half[t][:, block], step1[t][:, block], step2[t][:, b * P : (b + 1) * P])
-                        for i, term in enumerate(terms):
-                            nc.tensor.matmul(z_turned[b][:, t, :], term, ident[:], start=(i == 0), stop=(i == len(terms) - 1),
-                                             is_transpose=True)
+        def first_median_done(t):
+            turned = psum.tile([P, S], F32, name="turned", tag="bank")
+            for block in blocks:
+                turned_sum(turned[:, block], [y_own[t][:, block], step1[t][:, block]])
+            m1_turned = ring.tile([P, S], F32, name="m1_turned")
+            nc.scalar.copy(m1_turned[:], turned[:])
+            m1_back = psum.tile([P, S], F32, name="m1_back", tag="bank")
+            for block in blocks:
+                nc.tensor.transpose(m1_back[:, block], m1_turned[:, block], ident[:])
+            nc.scalar.copy(m1_win[t][:], m1_back[:])
+            nc.scalar.copy(m1_own[t][:], m1_back[:])
+            nc.scalar.activation(y_half[t][:], y_own[t][:], COPY, scale=-0.5)
+
+        def second_median_done(c, t):
+            for b in range(c * CHUNK // P, (c + 1) * CHUNK // P):
+                if t == 0:
+                    z_turned[b] = psum.tile([P, PACK, P], F32, name="z_turned", tag="bank")
+                turned_sum(z_turned[b][:, t, :], [y_half[t][:, blocks[b]], m1_own[t][:, blocks[b]], step2[t][:, blocks[b]]])
+            if t == PACK - 1:
+                second_product(c)
+
+        def second_product(c):
             z_back = psum.tile([P, CHUNK // P, 2, P], F32, name="z_back", tag="bank")
-            for b in range(CHUNK // P):
-                z_pairs = ring.tile([P, 2, P, 2], BF16, name="z_pairs")
+            for i in range(CHUNK // P):
+                b = c * CHUNK // P + i
+                z_pairs = keep.tile([P, 2, P, 2], BF16, name="z_pairs", tag="held" if b == len(blocks) - 1 else "z_pairs%d" % b)
                 nc.scalar.activation(z_pairs[:], z_turned[b][:].rearrange("j (u e) p -> j u p e", e=2), COPY, scale=-1.0)
                 z_words = z_pairs[:].rearrange("j u p e -> j u (p e)").bitcast(F32)
                 for u in range(2):
-                    nc.tensor.transpose(z_back[:, b, u, :], z_words[:, u, :], ident[:])
+                    nc.tensor.transpose(z_back[:, i, u, :], z_words[:, u, :], ident[:])
             z_bf = ring.tile([P, CHUNK * PACK], BF16, name="z_bf", align_bytes=64)
             nc.scalar.copy(z_bf[:].bitcast(F32).rearrange("p (b j u) -> p b j u", u=2, j=P),
                            z_back[:].rearrange("p b u j -> p b j u"))
             z_codes = ring.tile([P, CHUNK], U32, name="z_codes", align_bytes=64)
             z_bytes = ring.tile([P, CHUNK], U8, name="z_bytes", align_bytes=64)
             nc.vector.quantize_mx(z_codes[:].bitcast(FP8X4), z_bytes[:], z_bf[:])
+            if c == 1:
+                h[0, PACK - 1] = keep.tile([P, CHUNK], F32, name="h_held", tag="held")
+                nc.scalar.copy(h[0, PACK - 1][:], held_bank[0][:])
             for t in range(PACK):
                 bank = psum.tile([P, CHUNK], F32, name="bank", tag="bank")
                 nc.tensor.matmul_mx(bank[:], lhsT=w2_codes[:, t, :].bitcast(FP8X4), lhsT_scale=w2_bytes[:, t, :],
                                     rhs=z_codes[:].bitcast(FP8X4), rhs_scale=z_bytes[:], start=True, stop=True)
-                h[c, t] = keep.tile([P, CHUNK], F32, name="h%d_%d" % (c, t))
-                nc.scalar.copy(h[c, t][:], bank[:])
+                if (c, t) == (0, PACK - 1):
+                    held_bank.append(bank)
+                else:
+                    h[c, t] = keep.tile([P, CHUNK], F32, name="h%d_%d" % (c, t))
+                    nc.scalar.copy(h[c, t][:], bank[:])
+
+        jobs = [(y_win[t], y_own[t][:], p1_l[:], p2_l[:], step1[t][:], (first_median_done, t)) for t in range(PACK)]
+        for c, t in ((0, 0), (0, 1), (1, 0), (0, 2), (0, 3), (1, 1), (1, 2), (1, 3)):
+            cols = slice(c * CHUNK, (c + 1) * CHUNK)
+            entries = slice(c * CHUNK // 16, (c + 1) * CHUNK // 16)
+            jobs.append((m1_win[t], m1_own[t][:, cols], p3_l[:, entries], p4_l[:, entries], step2[t][:, cols],
+                         (second_median_done, c, t)))
+
+        for k in range(len(jobs) + 1):
+            if k < len(jobs):
+                window, own, list_a, list_b, step, follow = jobs[k]
+                nc.vector.tensor_tensor(diff_a[k % 2][:, : own.shape[1]], window[:].indirect(list_a), own, ALU.subtract)
+            if k > 0:
+                done_step, done_follow = jobs[k - 1][4:]
+                width, i = done_step.shape[1], (k - 1) % 2
+                nc.vector.scalar_tensor_tensor(low[i][:, :width], diff_b[i][:, :width], 0.0, diff_a[i][:, :width], ALU.min, ALU.max)
+            if k < len(jobs):
+                nc.vector.tensor_tensor(diff_b[k % 2][:, : own.shape[1]], window[:].indirect(list_b), own, ALU.subtract)
+            if k > 0:
+                nc.vector.scalar_tensor_tensor(done_step, diff_b[i][:, :width], 0.0, low[i][:, :width], ALU.max, ALU.min)
+                done_follow[0](*done_follow[1:])
 
         out_rows = out_0.rearrange("(p t) u -> p t u", t=PACK)
         rounded = keep.tile([P, PACK, U], BF16)
-        for c, t in ((0, 0), (0, 1), (0, 2), (1, 0), (1, 1), (1, 2), (0, 3), (1, 3)):
+        for c, t in ((0, 0), (0, 1), (0, 2), (0, 3), (1, 0), (1, 1), (1, 2), (1, 3)):
             entries = slice(c * CHUNK // 16, (c + 1) * CHUNK // 16)
             nc.vector.tensor_copy(page[t][:].indirect(slot_l[:, entries]), h[c, t][:])
             if c == 1:
@@ -194,9 +208,9 @@ def tile_picked_medfilt2_none_po_kernel(tc, x_words, x_scales, w1_words, w1_scal
                     nc.scalar.copy(rounded[:, t, VEC_COLS:], page[t][:, VEC_COLS:])
         grouped = keep.tile([P, U, PACK], BF16, align_bytes=64)
         half = U // 2
-        nc.vector.tensor_copy(grouped[:, :half, :], rounded[:, :, :half].rearrange("p t c -> p c t"))
-        nc.vector.tensor_copy(grouped[:, half:VEC_COLS, :], rounded[:, :, half:VEC_COLS].rearrange("p t c -> p c t"))
-        nc.scalar.copy(grouped[:, VEC_COLS:, :], rounded[:, :, VEC_COLS:].rearrange("p t c -> p c t"))
+        for copy, cols in ((nc.vector.tensor_copy, slice(0, half)), (nc.vector.tensor_copy, slice(half, VEC_COLS)),
+                           (nc.scalar.copy, slice(VEC_COLS, U))):
+            copy(grouped[:, cols, :].rearrange("p (c i) t -> p c t i", i=4), rounded[:, :, cols].rearrange("p t (c i) -> p c t i", i=4))
         out_codes = keep.tile([P, U], U32, align_bytes=64)
         out_bytes = keep.tile([P, U], U8, align_bytes=64)
         for cols in (slice(0, half), slice(half, U)):

@@ -15,12 +15,14 @@ U8 = mybir.dt.uint8
 FP8X4 = mybir.dt.float8_e4m3fn_x4
 ALU = mybir.AluOpType
 COPY = mybir.ActivationFunctionType.Copy
+RELU = mybir.ActivationFunctionType.Relu
 
 P = 128
 PACK = 4
 CHUNK = 256
 LIST_COLS = S // 16
-VEC_COLS = 576
+VEC_COLS = 608
+LIFTED = 2
 
 
 def tile_picked_medfilt2_none_po_kernel(tc, x_words, x_scales, w1_words, w1_scales, gn, w2_words, w2_scales, mem,
@@ -30,8 +32,9 @@ def tile_picked_medfilt2_none_po_kernel(tc, x_words, x_scales, w1_words, w1_scal
         lists = ctx.enter_context(tc.tile_pool(name="lists", bufs=1))
         keep = ctx.enter_context(tc.tile_pool(name="keep", bufs=1))
         shared = ctx.enter_context(tc.tile_pool(name="shared", bufs=1))
-        ring = ctx.enter_context(tc.tile_pool(name="ring", bufs=3))
-        psum = ctx.enter_context(tc.psum_pool(name="psum", bufs=8))
+        ring = ctx.enter_context(tc.tile_pool(name="ring", bufs=4))
+        psum = ctx.enter_context(tc.psum_pool(name="psum", bufs=3))
+        psum_one = ctx.enter_context(tc.psum_pool(name="psum_one", bufs=1))
 
         def load_list(src, name):
             tile = lists.tile([P, LIST_COLS], U16, name=name)
@@ -90,8 +93,6 @@ def tile_picked_medfilt2_none_po_kernel(tc, x_words, x_scales, w1_words, w1_scal
                                   x_table[:].bitcast(U32).indirect(offs_l[:, c * CHUNK // 16 : (c + 1) * CHUNK // 16]))
             if c == 0:
                 w1_bytes = deal(w1_plane, U8, "w1_bytes")
-        w2_codes = deal(w2_raw, I32, "w2_codes")
-        w2_bytes = deal(w2_plane, U8, "w2_bytes")
 
         y_own = [keep.tile([P, S], F32, name="y_own%d" % t) for t in range(PACK)]
         y_half = [keep.tile([P, S], F32, name="y_half%d" % t) for t in range(PACK)]
@@ -122,76 +123,103 @@ def tile_picked_medfilt2_none_po_kernel(tc, x_words, x_scales, w1_words, w1_scal
         diff_a = [keep.tile([P, S], F32, name="diff_a%d" % i) for i in range(2)]
         diff_b = [keep.tile([P, S], F32, name="diff_b%d" % i) for i in range(2)]
         low = [keep.tile([P, S], F32, name="low%d" % i) for i in range(2)]
+        below = {t: keep.tile([P, S], F32, name="below%d" % t) for t in range(LIFTED)}
         z_turned, h, held_bank = {}, {}, []
 
+        def turned_tile(terms, func, scale, tag):
+            bank = psum_one.tile([P, S], F32, name="bank", tag=tag)
+            for block in blocks:
+                turned_sum(bank[:, block], [term[:, block] for term in terms])
+            turned = ring.tile([P, S], F32, name="turned")
+            nc.scalar.activation(turned[:], bank[:], func, scale=scale)
+            return turned
+
         def first_median_done(t):
-            turned = psum.tile([P, S], F32, name="turned", tag="bank")
+            parts = [turned_tile([y_own[t], step1[t]], COPY, 1.0, "single" if t == LIFTED else "parity%d" % (t % 2))]
+            if t in below:
+                parts.append(turned_tile([step1[t], below[t]], RELU, -1.0, "single"))
+            m1_back = psum_one.tile([P, S], F32, name="m1_back", tag="parity%d" % (t % 2))
             for block in blocks:
-                turned_sum(turned[:, block], [y_own[t][:, block], step1[t][:, block]])
-            m1_turned = ring.tile([P, S], F32, name="m1_turned")
-            nc.scalar.copy(m1_turned[:], turned[:])
-            m1_back = psum.tile([P, S], F32, name="m1_back", tag="bank")
-            for block in blocks:
-                nc.tensor.transpose(m1_back[:, block], m1_turned[:, block], ident[:])
+                turned_sum(m1_back[:, block], [part[:, block] for part in parts])
             nc.scalar.copy(m1_win[t][:], m1_back[:])
             nc.scalar.copy(m1_own[t][:], m1_back[:])
-            nc.scalar.activation(y_half[t][:], y_own[t][:], COPY, scale=-0.5)
 
-        def second_median_done(c, t):
-            for b in range(c * CHUNK // P, (c + 1) * CHUNK // P):
-                if t == 0:
-                    z_turned[b] = psum.tile([P, PACK, P], F32, name="z_turned", tag="bank")
+        def second_median_done(cols, t):
+            if cols.start == 0:
+                nc.scalar.activation(y_half[t][:], y_own[t][:], COPY, scale=-0.5)
+            for b in range(cols.start // P, cols.stop // P):
+                if t == 0 and b < 2:
+                    two_banks = psum_one.tile([P, 2, PACK, P], F32, name="two_banks", tag="parity%d" % b)
+                    z_turned[b], z_turned[b + 2] = two_banks[:, 0, :, :], two_banks[:, 1, :, :]
                 turned_sum(z_turned[b][:, t, :], [y_half[t][:, blocks[b]], m1_own[t][:, blocks[b]], step2[t][:, blocks[b]]])
             if t == PACK - 1:
-                second_product(c)
+                second_product(cols.start // CHUNK)
 
         def second_product(c):
-            z_back = psum.tile([P, CHUNK // P, 2, P], F32, name="z_back", tag="bank")
+            z_bf = ring.tile([P, CHUNK // P, P * PACK], BF16, name="z_bf", align_bytes=64)
             for i in range(CHUNK // P):
                 b = c * CHUNK // P + i
-                z_pairs = keep.tile([P, 2, P, 2], BF16, name="z_pairs", tag="held" if b == len(blocks) - 1 else "z_pairs%d" % b)
-                nc.scalar.activation(z_pairs[:], z_turned[b][:].rearrange("j (u e) p -> j u p e", e=2), COPY, scale=-1.0)
+                z_pairs = ring.tile([P, 2, P, 2], BF16, name="z_pairs")
+                nc.scalar.activation(z_pairs[:], z_turned[b].rearrange("j (u e) p -> j u p e", e=2), COPY, scale=-1.0)
                 z_words = z_pairs[:].rearrange("j u p e -> j u (p e)").bitcast(F32)
+                if b == len(blocks) - 1:
+                    z_back = held_bank[0][:, CHUNK:]
+                else:
+                    own_bank = psum.tile([P, 2 * P], F32, name="own_bank", tag="bank")
+                    z_back = own_bank[:]
                 for u in range(2):
-                    nc.tensor.transpose(z_back[:, i, u, :], z_words[:, u, :], ident[:])
-            z_bf = ring.tile([P, CHUNK * PACK], BF16, name="z_bf", align_bytes=64)
-            nc.scalar.copy(z_bf[:].bitcast(F32).rearrange("p (b j u) -> p b j u", u=2, j=P),
-                           z_back[:].rearrange("p b u j -> p b j u"))
+                    nc.tensor.transpose(z_back[:, u * P : (u + 1) * P], z_words[:, u, :], ident[:])
+                nc.scalar.copy(z_bf[:, i, :].bitcast(F32).rearrange("p (j u) -> p j u", u=2), z_back.rearrange("p (u j) -> p j u", u=2))
             z_codes = ring.tile([P, CHUNK], U32, name="z_codes", align_bytes=64)
             z_bytes = ring.tile([P, CHUNK], U8, name="z_bytes", align_bytes=64)
-            nc.vector.quantize_mx(z_codes[:].bitcast(FP8X4), z_bytes[:], z_bf[:])
+            nc.vector.quantize_mx(z_codes[:].bitcast(FP8X4), z_bytes[:], z_bf[:].rearrange("p i k -> p (i k)"))
             if c == 1:
-                h[0, PACK - 1] = keep.tile([P, CHUNK], F32, name="h_held", tag="held")
-                nc.scalar.copy(h[0, PACK - 1][:], held_bank[0][:])
+                nc.scalar.copy(h[0, PACK - 1][:], held_bank[0][:, :CHUNK])
             for t in range(PACK):
-                bank = psum.tile([P, CHUNK], F32, name="bank", tag="bank")
-                nc.tensor.matmul_mx(bank[:], lhsT=w2_codes[:, t, :].bitcast(FP8X4), lhsT_scale=w2_bytes[:, t, :],
-                                    rhs=z_codes[:].bitcast(FP8X4), rhs_scale=z_bytes[:], start=True, stop=True)
-                if (c, t) == (0, PACK - 1):
+                h[c, t] = keep.tile([P, CHUNK], F32, name="h%d_%d" % (c, t))
+                held = (c, t) == (0, PACK - 1)
+                if held:
+                    bank = psum_one.tile([P, CHUNK + 2 * P], F32, name="bank", tag="single")
                     held_bank.append(bank)
                 else:
-                    h[c, t] = keep.tile([P, CHUNK], F32, name="h%d_%d" % (c, t))
+                    bank = psum.tile([P, CHUNK], F32, name="bank", tag="bank")
+                nc.tensor.matmul_mx(bank[:, :CHUNK], lhsT=w2_codes[:, t, :].bitcast(FP8X4), lhsT_scale=w2_bytes[:, t, :],
+                                    rhs=z_codes[:].bitcast(FP8X4), rhs_scale=z_bytes[:], start=True, stop=True)
+                if not held:
                     nc.scalar.copy(h[c, t][:], bank[:])
 
         jobs = [(y_win[t], y_own[t][:], p1_l[:], p2_l[:], step1[t][:], (first_median_done, t)) for t in range(PACK)]
-        for c, t in ((0, 0), (0, 1), (1, 0), (0, 2), (0, 3), (1, 1), (1, 2), (1, 3)):
-            cols = slice(c * CHUNK, (c + 1) * CHUNK)
-            entries = slice(c * CHUNK // 16, (c + 1) * CHUNK // 16)
+        chunks = [slice(c * CHUNK, (c + 1) * CHUNK) for c in range(S // CHUNK)]
+        for cols, t in [(chunk, t) for chunk in chunks for t in range(PACK)]:
+            entries = slice(cols.start // 16, cols.stop // 16)
             jobs.append((m1_win[t], m1_own[t][:, cols], p3_l[:, entries], p4_l[:, entries], step2[t][:, cols],
-                         (second_median_done, c, t)))
+                         (second_median_done, cols, t)))
 
         for k in range(len(jobs) + 1):
+            if k == PACK + 1:
+                w2_codes = deal(w2_raw, I32, "w2_codes")
+                w2_bytes = deal(w2_plane, U8, "w2_bytes")
             if k < len(jobs):
                 window, own, list_a, list_b, step, follow = jobs[k]
-                nc.vector.tensor_tensor(diff_a[k % 2][:, : own.shape[1]], window[:].indirect(list_a), own, ALU.subtract)
+                if k == 0:
+                    for chunk in chunks:
+                        nc.vector.tensor_tensor(diff_a[0][:, chunk], window[:].indirect(list_a[:, chunk.start // 16 : chunk.stop // 16]),
+                                                own[:, chunk], ALU.subtract)
+                else:
+                    nc.vector.tensor_tensor(diff_a[k % 2][:, : own.shape[1]], window[:].indirect(list_a), own, ALU.subtract)
             if k > 0:
                 done_step, done_follow = jobs[k - 1][4:]
                 width, i = done_step.shape[1], (k - 1) % 2
-                nc.vector.scalar_tensor_tensor(low[i][:, :width], diff_b[i][:, :width], 0.0, diff_a[i][:, :width], ALU.min, ALU.max)
+                capped = done_step if k - 1 in below else low[i][:, :width]
+                nc.vector.scalar_tensor_tensor(capped, diff_b[i][:, :width], 0.0, diff_a[i][:, :width], ALU.max, ALU.min)
+                if k - 1 in below:
+                    done_follow[0](*done_follow[1:])
             if k < len(jobs):
                 nc.vector.tensor_tensor(diff_b[k % 2][:, : own.shape[1]], window[:].indirect(list_b), own, ALU.subtract)
-            if k > 0:
-                nc.vector.scalar_tensor_tensor(done_step, diff_b[i][:, :width], 0.0, low[i][:, :width], ALU.max, ALU.min)
+                if k in below:
+                    nc.scalar.activation(below[k][:], diff_b[k % 2][:], RELU, scale=-1.0)
+            if k > 0 and k - 1 not in below:
+                nc.vector.scalar_tensor_tensor(done_step, diff_b[i][:, :width], 0.0, capped, ALU.min, ALU.max)
                 done_follow[0](*done_follow[1:])
 
         out_rows = out_0.rearrange("(p t) u -> p t u", t=PACK)

from contextlib import ExitStack

import concourse.mybir as mybir
from concourse.masks import make_identity

K, T, S, N, H, U = 512, 2048, 512, 512, 512, 1024
FLOPS = 2 * K * H * S + 2 * H * N * S

F32 = mybir.dt.float32
BF16 = mybir.dt.bfloat16
I32 = mybir.dt.int32
U32 = mybir.dt.uint32
U16 = mybir.dt.uint16
U8 = mybir.dt.uint8
FP8X4 = mybir.dt.float8_e4m3fn_x4
ALU = mybir.AluOpType
COPY = mybir.ActivationFunctionType.Copy
RELU = mybir.ActivationFunctionType.Relu

P = 128
PACK = 4
CHUNK = 256
LIST_COLS = S // 16
VEC_COLS = 608
LIFTED = 2


def tile_picked_medfilt2_none_po_kernel(tc, x_words, x_scales, w1_words, w1_scales, gn, w2_words, w2_scales, mem,
        offs, p1, p2, p3, p4, slot, out_0, out_1, out_2):
    nc = tc.nc
    with ExitStack() as ctx:
        lists = ctx.enter_context(tc.tile_pool(name="lists", bufs=1))
        keep = ctx.enter_context(tc.tile_pool(name="keep", bufs=1))
        shared = ctx.enter_context(tc.tile_pool(name="shared", bufs=1))
        ring = ctx.enter_context(tc.tile_pool(name="ring", bufs=4))
        psum = ctx.enter_context(tc.psum_pool(name="psum", bufs=3))
        psum_one = ctx.enter_context(tc.psum_pool(name="psum_one", bufs=1))

        def load_list(src, name):
            tile = lists.tile([P, LIST_COLS], U16, name=name)
            nc.sync.dma_start(tile[:], src)
            return tile

        def load_scales(src, plane, queues):
            for q, queue in enumerate(queues):
                queue.dma_start(plane[32 * q : 32 * q + 4, :].bitcast(I32), src[0, 4 * q : 4 * q + 4, :].bitcast(I32))

        def words_of(src):
            return src[0].rearrange("p n t -> p (n t)").bitcast(I32)

        def deal(raw, dtype, name):
            dealt = keep.tile([P, PACK, P], dtype, name=name, align_bytes=64)
            nc.vector.tensor_copy(dealt[:], raw[:].rearrange("p (m t) -> p t m", t=PACK))
            return dealt

        offs_l = load_list(offs, "offs_l")
        p1_l = load_list(p1, "p1_l")
        p2_l = load_list(p2, "p2_l")
        p3_l = load_list(p3, "p3_l")
        p4_l = load_list(p4, "p4_l")
        slot_l = load_list(slot, "slot_l")
        gain = keep.tile([P, PACK], F32)
        nc.sync.dma_start(gain[:], gn.rearrange("(p t) o -> p (t o)", t=PACK))
        w1_raw = keep.tile([P, H], I32)
        nc.sync.dma_start(w1_raw[:], words_of(w1_words))
        x_plane = keep.tile([P, T], U8)
        nc.vector.memset(x_plane[:].bitcast(I32), 0)
        load_scales(x_scales, x_plane, [nc.sync] * 4)
        x_table = shared.tile([P, T], I32, offset=2048)
        nc.sync.dma_start(x_table[:], words_of(x_words))
        w1_plane = keep.tile([P, H], U8)
        nc.gpsimd.memset(w1_plane[:].bitcast(I32), 0)
        load_scales(w1_scales, w1_plane, [nc.sync] * 4)
        w2_raw = keep.tile([P, N], I32)
        nc.sync.dma_start(w2_raw[:], words_of(w2_words))
        w2_plane = keep.tile([P, N], U8)
        nc.vector.memset(w2_plane[:].bitcast(I32), 0)
        load_scales(w2_scales, w2_plane, [nc.sync] * 4)

        y_win = [keep.tile([P, 2 * S], F32, name="y_win%d" % t) for t in range(PACK)]
        nc.vector.memset(y_win[0][:, S:], 0.0)
        for t in range(1, PACK):
            nc.scalar.activation(y_win[t][:, S:], y_win[0][:, S:], COPY)
        ident = keep.tile([P, P], F32)
        make_identity(nc, ident[:])

        w1_codes = deal(w1_raw, I32, "w1_codes")
        x_bytes = keep.tile([P, S], U8, align_bytes=64)
        nc.vector.tensor_copy(x_bytes[:], x_plane[:].indirect(offs_l[:]))
        x_codes = shared.tile([P, S], U32, offset=12288, align_bytes=64)
        for c in range(S // CHUNK):
            nc.vector.tensor_copy(x_codes[:, c * CHUNK : (c + 1) * CHUNK],
                                  x_table[:].bitcast(U32).indirect(offs_l[:, c * CHUNK // 16 : (c + 1) * CHUNK // 16]))
            if c == 0:
                w1_bytes = deal(w1_plane, U8, "w1_bytes")

        y_own = [keep.tile([P, S], F32, name="y_own%d" % t) for t in range(PACK)]
        y_half = [keep.tile([P, S], F32, name="y_half%d" % t) for t in range(PACK)]
        for t in range(PACK):
            width = CHUNK if t == 0 else S
            for c in range(S // width):
                cols = slice(c * width, (c + 1) * width)
                bank = psum.tile([P, width], F32, name="bank", tag="bank")
                nc.tensor.matmul_mx(bank[:], lhsT=w1_codes[:, t, :].bitcast(FP8X4), lhsT_scale=w1_bytes[:, t, :],
                                    rhs=x_codes[:, cols].bitcast(FP8X4), rhs_scale=x_bytes[:, cols], start=True, stop=True)
                nc.scalar.activation(y_win[t][:, cols], bank[:], COPY, scale=gain[:, t : t + 1])
                nc.scalar.activation(y_own[t][:, cols], bank[:], COPY, scale=gain[:, t : t + 1])

        page = [shared.tile([P, U], F32, name="page%d" % t, offset=4096 * t) for t in range(PACK)]
        mem_rows = mem.rearrange("(p t) u -> p t u", t=PACK)
        for t in range(PACK):
            nc.sync.dma_start(page[t][:], mem_rows[:, t, :])

        def turned_sum(out, terms):
            for i, term in enumerate(terms):
                nc.tensor.matmul(out, term, ident[:], start=(i == 0), stop=(i == len(terms) - 1), is_transpose=True)

        blocks = [slice(b * P, (b + 1) * P) for b in range(S // P)]
        m1_win = [keep.tile([P, S], F32, name="m1_win%d" % t) for t in range(PACK)]
        m1_own = [keep.tile([P, S], F32, name="m1_own%d" % t) for t in range(PACK)]
        step1 = [keep.tile([P, S], F32, name="step1_%d" % t) for t in range(PACK)]
        step2 = [keep.tile([P, S], F32, name="step2_%d" % t) for t in range(PACK)]
        diff_a = [keep.tile([P, S], F32, name="diff_a%d" % i) for i in range(2)]
        diff_b = [keep.tile([P, S], F32, name="diff_b%d" % i) for i in range(2)]
        low = [keep.tile([P, S], F32, name="low%d" % i) for i in range(2)]
        below = {t: keep.tile([P, S], F32, name="below%d" % t) for t in range(LIFTED)}
        z_turned, h, held_bank = {}, {}, []

        def turned_tile(terms, func, scale, tag):
            bank = psum_one.tile([P, S], F32, name="bank", tag=tag)
            for block in blocks:
                turned_sum(bank[:, block], [term[:, block] for term in terms])
            turned = ring.tile([P, S], F32, name="turned")
            nc.scalar.activation(turned[:], bank[:], func, scale=scale)
            return turned

        def first_median_done(t):
            parts = [turned_tile([y_own[t], step1[t]], COPY, 1.0, "single" if t == LIFTED else "parity%d" % (t % 2))]
            if t in below:
                parts.append(turned_tile([step1[t], below[t]], RELU, -1.0, "single"))
            m1_back = psum_one.tile([P, S], F32, name="m1_back", tag="parity%d" % (t % 2))
            for block in blocks:
                turned_sum(m1_back[:, block], [part[:, block] for part in parts])
            nc.scalar.copy(m1_win[t][:], m1_back[:])
            nc.scalar.copy(m1_own[t][:], m1_back[:])

        def second_median_done(cols, t):
            if cols.start == 0:
                nc.scalar.activation(y_half[t][:], y_own[t][:], COPY, scale=-0.5)
            for b in range(cols.start // P, cols.stop // P):
                if t == 0 and b < 2:
                    two_banks = psum_one.tile([P, 2, PACK, P], F32, name="two_banks", tag="parity%d" % b)
                    z_turned[b], z_turned[b + 2] = two_banks[:, 0, :, :], two_banks[:, 1, :, :]
                turned_sum(z_turned[b][:, t, :], [y_half[t][:, blocks[b]], m1_own[t][:, blocks[b]], step2[t][:, blocks[b]]])
            if t == PACK - 1:
                second_product(cols.start // CHUNK)

        def second_product(c):
            z_bf = ring.tile([P, CHUNK // P, P * PACK], BF16, name="z_bf", align_bytes=64)
            for i in range(CHUNK // P):
                b = c * CHUNK // P + i
                z_pairs = ring.tile([P, 2, P, 2], BF16, name="z_pairs")
                nc.scalar.activation(z_pairs[:], z_turned[b].rearrange("j (u e) p -> j u p e", e=2), COPY, scale=-1.0)
                z_words = z_pairs[:].rearrange("j u p e -> j u (p e)").bitcast(F32)
                if b == len(blocks) - 1:
                    z_back = held_bank[0][:, CHUNK:]
                else:
                    own_bank = psum.tile([P, 2 * P], F32, name="own_bank", tag="bank")
                    z_back = own_bank[:]
                for u in range(2):
                    nc.tensor.transpose(z_back[:, u * P : (u + 1) * P], z_words[:, u, :], ident[:])
                nc.scalar.copy(z_bf[:, i, :].bitcast(F32).rearrange("p (j u) -> p j u", u=2), z_back.rearrange("p (u j) -> p j u", u=2))
            z_codes = ring.tile([P, CHUNK], U32, name="z_codes", align_bytes=64)
            z_bytes = ring.tile([P, CHUNK], U8, name="z_bytes", align_bytes=64)
            nc.vector.quantize_mx(z_codes[:].bitcast(FP8X4), z_bytes[:], z_bf[:].rearrange("p i k -> p (i k)"))
            if c == 1:
                nc.scalar.copy(h[0, PACK - 1][:], held_bank[0][:, :CHUNK])
            for t in range(PACK):
                h[c, t] = keep.tile([P, CHUNK], F32, name="h%d_%d" % (c, t))
                held = (c, t) == (0, PACK - 1)
                if held:
                    bank = psum_one.tile([P, CHUNK + 2 * P], F32, name="bank", tag="single")
                    held_bank.append(bank)
                else:
                    bank = psum.tile([P, CHUNK], F32, name="bank", tag="bank")
                nc.tensor.matmul_mx(bank[:, :CHUNK], lhsT=w2_codes[:, t, :].bitcast(FP8X4), lhsT_scale=w2_bytes[:, t, :],
                                    rhs=z_codes[:].bitcast(FP8X4), rhs_scale=z_bytes[:], start=True, stop=True)
                if not held:
                    nc.scalar.copy(h[c, t][:], bank[:])

        jobs = [(y_win[t], y_own[t][:], p1_l[:], p2_l[:], step1[t][:], (first_median_done, t)) for t in range(PACK)]
        chunks = [slice(c * CHUNK, (c + 1) * CHUNK) for c in range(S // CHUNK)]
        for cols, t in [(chunk, t) for chunk in chunks for t in range(PACK)]:
            entries = slice(cols.start // 16, cols.stop // 16)
            jobs.append((m1_win[t], m1_own[t][:, cols], p3_l[:, entries], p4_l[:, entries], step2[t][:, cols],
                         (second_median_done, cols, t)))

        for k in range(len(jobs) + 1):
            if k == PACK + 1:
                w2_codes = deal(w2_raw, I32, "w2_codes")
                w2_bytes = deal(w2_plane, U8, "w2_bytes")
            if k < len(jobs):
                window, own, list_a, list_b, step, follow = jobs[k]
                if k == 0:
                    for chunk in chunks:
                        nc.vector.tensor_tensor(diff_a[0][:, chunk], window[:].indirect(list_a[:, chunk.start // 16 : chunk.stop // 16]),
                                                own[:, chunk], ALU.subtract)
                else:
                    nc.vector.tensor_tensor(diff_a[k % 2][:, : own.shape[1]], window[:].indirect(list_a), own, ALU.subtract)
            if k > 0:
                done_step, done_follow = jobs[k - 1][4:]
                width, i = done_step.shape[1], (k - 1) % 2
                capped = done_step if k - 1 in below else low[i][:, :width]
                nc.vector.scalar_tensor_tensor(capped, diff_b[i][:, :width], 0.0, diff_a[i][:, :width], ALU.max, ALU.min)
                if k - 1 in below:
                    done_follow[0](*done_follow[1:])
            if k < len(jobs):
                nc.vector.tensor_tensor(diff_b[k % 2][:, : own.shape[1]], window[:].indirect(list_b), own, ALU.subtract)
                if k in below:
                    nc.scalar.activation(below[k][:], diff_b[k % 2][:], RELU, scale=-1.0)
            if k > 0 and k - 1 not in below:
                nc.vector.scalar_tensor_tensor(done_step, diff_b[i][:, :width], 0.0, capped, ALU.min, ALU.max)
                done_follow[0](*done_follow[1:])

        out_rows = out_0.rearrange("(p t) u -> p t u", t=PACK)
        rounded = keep.tile([P, PACK, U], BF16)
        for c, t in ((0, 0), (0, 1), (0, 2), (0, 3), (1, 0), (1, 1), (1, 2), (1, 3)):
            entries = slice(c * CHUNK // 16, (c + 1) * CHUNK // 16)
            nc.vector.tensor_copy(page[t][:].indirect(slot_l[:, entries]), h[c, t][:])
            if c == 1:
                nc.sync.dma_start(out_rows[:, t, :], page[t][:])
                if t < PACK - 1:
                    nc.scalar.copy(rounded[:, t, :], page[t][:])
                else:
                    nc.vector.tensor_copy(rounded[:, t, :VEC_COLS], page[t][:, :VEC_COLS])
                    nc.scalar.copy(rounded[:, t, VEC_COLS:], page[t][:, VEC_COLS:])
        grouped = keep.tile([P, U, PACK], BF16, align_bytes=64)
        half = U // 2
        for copy, cols in ((nc.vector.tensor_copy, slice(0, half)), (nc.vector.tensor_copy, slice(half, VEC_COLS)),
                           (nc.scalar.copy, slice(VEC_COLS, U))):
            copy(grouped[:, cols, :].rearrange("p (c i) t -> p c t i", i=4), rounded[:, :, cols].rearrange("p t (c i) -> p c t i", i=4))
        out_codes = keep.tile([P, U], U32, align_bytes=64)
        out_bytes = keep.tile([P, U], U8, align_bytes=64)
        for cols in (slice(0, half), slice(half, U)):
            nc.vector.quantize_mx(out_codes[:, cols].bitcast(FP8X4), out_bytes[:, cols],
                                  grouped[:, cols, :].rearrange("p c t -> p (c t)"))
            nc.sync.dma_start(words_of(out_1)[:, cols], out_codes[:, cols].bitcast(I32))
        for q in range(4):
            nc.scalar.dma_start(out_2[0, 4 * q : 4 * q + 4, :].bitcast(I32), out_bytes[32 * q : 32 * q + 4, :].bitcast(I32))
